import numpy as np
import ml_dtypes


def mxq(x, axis, fmt="e4m3"):
    dtype, down = {"e4m3": (ml_dtypes.float8_e4m3fn, 7), "e5m2": (ml_dtypes.float8_e5m2, 14)}[fmt]
    v = np.moveaxis(np.asarray(x, np.float32).astype(ml_dtypes.bfloat16).astype(np.float64), axis, -1)
    blocks = v.reshape(v.shape[:-1] + (-1, 32))
    amax = np.abs(blocks).max(-1, keepdims=True)
    byte = np.maximum(np.where(amax > 0, np.frexp(amax)[1] - 1 + 127, 0) - down, 1)
    scale = np.exp2(byte - 127.0)
    codes = (blocks / scale).astype(np.float32).astype(dtype).astype(np.float64)
    return np.moveaxis((codes * scale).reshape(v.shape), -1, axis)


WIDE = False


def mx_kscale(k):
    if not WIDE:
        return np.ones(k)
    levels = np.array([10, -10, 5, -5, 0])
    if k % 512:
        return np.exp2(np.random.permutation(np.resize(levels, k // 32))).repeat(32)
    a = np.empty((k // 512, 16))
    for p in range(k // 512):
        a[p, :8] = np.random.permutation(np.resize(levels, 8))
        for g in range(8):
            far = levels[np.abs(levels - a[p, g]) >= 10]
            a[p, g + 8] = far[np.random.randint(len(far))]
    return np.exp2(a.ravel()).repeat(32)


def f64(x):
    return np.asarray(x).astype(np.float64)


def striped(idx):
    return np.tile(np.asarray(idx).reshape(-1, 16).T, (8, 1)).astype(np.uint16)


def unstriped(offs):
    return offs[:16].T.reshape(-1).astype(np.int64)


def striped8(idx):
    return np.asarray(idx).reshape(8, -1, 16).transpose(0, 2, 1).reshape(128, -1).astype(np.uint16)


def unstriped8(offs):
    return offs.reshape(8, 16, -1).transpose(0, 2, 1).reshape(8, -1).astype(np.int64)


def pick8(x, idx, run):
    r = np.arange(len(x))
    return x[r[:, None], idx[r % (8 * run) // run]]


E2M1 = np.array([0.0, 0.5, 1.0, 1.5, 2.0, 3.0, 4.0, 6.0, -0.0, -0.5, -1.0, -1.5, -2.0, -3.0, -4.0, -6.0])


def pack_weight(w, fmt):
    k, n = w.shape
    w = f64(np.asarray(w, np.float32).astype(ml_dtypes.bfloat16)).reshape(k // 32, 32, n)
    amax = np.abs(w).max(1)
    if fmt == "e4m3":
        byte = np.frexp(amax)[1] - 1 + 127 - 7
    else:
        mant, ex = np.frexp(amax / 6.0)
        byte = np.where(mant > 0.5, ex, ex - 1) + 127
    byte = np.clip(np.where(amax > 0, byte, 1), 1, 254)
    scaled = (w * np.exp2(127.0 - byte)[:, None, :]).reshape(k, n).astype(np.float32)
    by_word = np.ascontiguousarray(scaled.reshape(k // 512, 128, 4, n).transpose(0, 1, 3, 2))
    if fmt == "e4m3":
        words = by_word.astype(ml_dtypes.float8_e4m3fn).view(np.uint8)
    else:
        c = by_word.astype(ml_dtypes.float4_e2m1fn).view(np.uint8) & 0xF
        words = (c[..., 0::2] | (c[..., 1::2] << 4)).reshape(k // 512, 128, 2 * n)
    return np.ascontiguousarray(words), np.ascontiguousarray(byte.astype(np.uint8).reshape(k // 512, 16, n))


def unpack_weight(words, scales, fmt):
    g, _, n = scales.shape
    words = np.ascontiguousarray(words).reshape(g, 128, n, -1)
    if fmt == "e4m3":
        vals = words.view(ml_dtypes.float8_e4m3fn).astype(np.float64)
    else:
        nib = np.empty((g, 128, n, 4), np.uint8)
        nib[..., 0::2] = words & 0xF
        nib[..., 1::2] = words >> 4
        vals = E2M1[nib]
    vals = vals * np.repeat(np.exp2(scales.astype(np.float64) - 127.0), 8, axis=1)[..., None]
    return vals.transpose(0, 1, 3, 2).reshape(g * 512, n)


def sigmoid(v):
    return 1.0 / (1.0 + np.exp(-v))


K, R, F, T, J, U = 512, 128, 512, 2048, 512, 1024


def setup_inputs():
    n = np.random.standard_normal
    idx = np.random.permutation(T)[:J]
    idx2 = np.stack([np.random.permutation(U)[:J] for _ in range(8)])
    fk = mx_kscale(K)
    dtabp = pack_weight(n((K, T)) / fk[:, None], "e2m1")
    tabp = pack_weight(n((K, T)) / fk[:, None], "e2m1")
    return {
        "dtab_words": dtabp[0],
        "dtab_scales": dtabp[1],
        "tab_words": tabp[0],
        "tab_scales": tabp[1],
        "w1": (n((K, R)) * 1 / np.sqrt(K) * fk[:, None]).astype(np.float32),
        "gain": (np.random.uniform(0.5, 1.5, (R, 1))).astype(np.float32),
        "ground": (n((R, U)) * 1.0).astype(np.float32),
        "og": (np.random.uniform(0.5, 2.0, (R, 1))).astype(np.float32),
        "base": (0.3 * n((R, U))).astype(np.float32),
        "offs": striped(idx),
        "offs2": striped8(idx2),
    }


def reference(dtab_words, dtab_scales, tab_words, tab_scales, w1, gain, ground, og, base, offs, offs2):
    idx = unstriped(offs)
    idx2 = unstriped8(offs2)
    dtabu = unpack_weight(dtab_words, dtab_scales, "e2m1")
    tabu = unpack_weight(tab_words, tab_scales, "e2m1")
    w1q = mxq(f64(w1), 0, "e4m3")
    tabidxg = tabu[:, idx]
    a = w1q.T @ tabidxg
    dtabidxg = dtabu[:, idx]
    ta = w1q.T @ dtabidxg
    h1 = a * f64(gain)
    pg = np.zeros((R, U))
    pg[np.arange(R)[:, None], idx2[np.arange(R) % 128 // 16]] = h1
    gt = sigmoid(pg)
    xh1 = ta * f64(gain)
    xpg = np.zeros((R, U))
    xpg[np.arange(R)[:, None], idx2[np.arange(R) % 128 // 16]] = xh1
    xgt = xpg * gt * (1.0 - gt)
    xu1 = xpg + xgt * f64(ground)
    y = xu1 * f64(og) + f64(base)
    return y

@@ -1,0 +1,121 @@
+from contextlib import ExitStack
+
+import concourse.mybir as mybir
+
+K, R, T, J, U = 512, 128, 2048, 512, 1024
+FLOPS = 2 * 2 * K * R * J
+
+F32 = mybir.dt.float32
+BF16 = mybir.dt.bfloat16
+I32 = mybir.dt.int32
+U32 = mybir.dt.uint32
+U16 = mybir.dt.uint16
+U8 = mybir.dt.uint8
+FP8X4 = mybir.dt.float8_e4m3fn_x4
+FP4X4 = mybir.dt.float4_e2m1fn_x4
+ACT = mybir.ActivationFunctionType
+ALU = mybir.AluOpType
+P = 128
+H = J // 2
+C = 256
+
+
+def tile_attend_tcgroundgate_kernel(tc, dtab_words, dtab_scales, tab_words, tab_scales, w1, gain, ground, og, base, offs, offs2, out):
+    nc = tc.nc
+    with ExitStack() as ctx:
+        sb = ctx.enter_context(tc.tile_pool(name="sb", bufs=1))
+        ps = ctx.enter_context(tc.psum_pool(name="ps", bufs=1))
+
+        offs_t = sb.tile([P, J // 16], U16, name="offs_t")
+        offs2_t = sb.tile([P, J // 16], U16, name="offs2_t")
+        tw = sb.tile([P, T], U16, name="tw")
+        dw = sb.tile([P, T], U16, name="dw")
+        ts = sb.tile([P, T], U8, name="ts")
+        ds = sb.tile([P, T], U8, name="ds")
+        w_raw = sb.tile([P, 4, R], F32, name="w_raw")
+        gain_t = sb.tile([P, 1], F32, name="gain_t")
+        og_t = sb.tile([P, 1], F32, name="og_t")
+        ground_t = sb.tile([P, U], F32, name="ground_t")
+        base_t = sb.tile([P, U], F32, name="base_t")
+        page_a = sb.tile([P, U], F32, name="page_a")
+        page_b = sb.tile([P, U], F32, name="page_b")
+
+        nc.vector.memset(ts[:].bitcast(I32), 0)
+        nc.vector.memset(ds[:].bitcast(I32), 0)
+        nc.vector.memset(page_b[:], 0.0)
+        nc.vector.memset(page_a[:], 0.0)
+
+        nc.sync.dma_start(offs_t[:], offs)
+        nc.sync.dma_start(tw[:].bitcast(I32), tab_words[0].bitcast(I32))
+        nc.sync.dma_start(w_raw[:], w1.rearrange("(p j) r -> p j r", j=4))
+        for q in range(4):
+            nc.scalar.dma_start(ts[32 * q : 32 * q + 4, :].bitcast(I32), tab_scales[0, 4 * q : 4 * q + 4, :].bitcast(I32))
+        nc.sync.dma_start(dw[:].bitcast(I32), dtab_words[0].bitcast(I32))
+        nc.gpsimd.dma_start(gain_t[:], gain)
+        nc.gpsimd.dma_start(og_t[:], og)
+        for q in range(4):
+            nc.sync.dma_start(ds[32 * q : 32 * q + 4, :].bitcast(I32), dtab_scales[0, 4 * q : 4 * q + 4, :].bitcast(I32))
+        nc.sync.dma_start(offs2_t[:], offs2)
+        nc.sync.dma_start(ground_t[:], ground)
+        nc.sync.dma_start(base_t[:], base)
+
+        w_bf = sb.tile([P, R, 4], BF16, name="w_bf", align_bytes=64)
+        w_q = sb.tile([P, R], U32, name="w_q", align_bytes=64)
+        w_s = sb.tile([P, R], U8, name="w_s", align_bytes=64)
+        nc.scalar.copy(w_bf[:], w_raw[:].rearrange("p j r -> p r j"))
+        gg = sb.tile([P, 1], F32, name="gg")
+        nc.gpsimd.tensor_tensor(gg[:], gain_t[:], og_t[:], ALU.mult)
+
+        gts = sb.tile([P, J], U8, name="gts", align_bytes=64)
+        gtw = sb.tile([P, J], U16, name="gtw", align_bytes=64)
+        nc.vector.tensor_copy(gts[:], ts[:].indirect(offs_t[:]))
+        nc.vector.tensor_copy(gtw[:], tw[:].indirect(offs_t[:]))
+        nc.vector.quantize_mx(out=w_q[:].bitcast(FP8X4), scales=w_s[:], in_=w_bf[:].rearrange("p r j -> p (r j)"))
+        acc_a = ps.tile([P, J], F32, name="acc_a")
+        nc.tensor.matmul_mx(out=acc_a[:], lhsT=w_q[:].bitcast(FP8X4), lhsT_scale=w_s[:], rhs=gtw[:].bitcast(FP4X4), rhs_scale=gts[:], start=True, stop=True)
+        sig = sb.tile([P, J], F32, name="sig")
+        sq = sb.tile([P, J], F32, name="sq")
+        slope = sb.tile([P, J], F32, name="slope")
+        nc.scalar.activation(sig[:], acc_a[:], ACT.Sigmoid, scale=gain_t[:])
+        nc.scalar.activation(sq[:], sig[:], ACT.Square, bias=-0.5)
+        nc.scalar.activation(slope[:], sq[:], ACT.Copy, scale=-1.0, bias=0.25)
+
+        xa = sb.tile([P, J], F32, name="xa")
+        for h in range(2):
+            cols = slice(h * H // 16, (h + 1) * H // 16)
+            gds = sb.tile([P, H], U8, name="gds%d" % h, align_bytes=64)
+            gdw = sb.tile([P, H], U16, name="gdw%d" % h, align_bytes=64)
+            nc.vector.tensor_copy(gds[:], ds[:].indirect(offs_t[:, cols]))
+            nc.vector.tensor_copy(gdw[:], dw[:].indirect(offs_t[:, cols]))
+            acc_d = ps.tile([P, H], F32, name="acc_d%d" % h)
+            nc.tensor.matmul_mx(out=acc_d[:], lhsT=w_q[:].bitcast(FP8X4), lhsT_scale=w_s[:], rhs=gdw[:].bitcast(FP4X4), rhs_scale=gds[:], start=True, stop=True)
+            nc.scalar.activation(xa[:, h * H : (h + 1) * H], acc_d[:], ACT.Copy, scale=gg[:])
+
+        for h in range(2):
+            cols = slice(h * H // 16, (h + 1) * H // 16)
+            nc.vector.tensor_tensor(page_b[:].indirect(offs2_t[:, cols]), xa[:, h * H : (h + 1) * H], slope[:, h * H : (h + 1) * H], ALU.mult)
+        nc.vector.tensor_copy(page_a[:].indirect(offs2_t[:]), xa[:])
+
+        prod = [sb.tile([P, C], F32, name="prod%d" % c) for c in range(4)]
+        part = [sb.tile([P, C], F32, name="part%d" % c) for c in range(4)]
+        res = [sb.tile([P, C], F32, name="res%d" % c) for c in range(4)]
+
+        def mul(eng, c):
+            eng.tensor_tensor(prod[c][:], page_b[:, c * C : (c + 1) * C], ground_t[:, c * C : (c + 1) * C], ALU.mult)
+
+        def addb(eng, c):
+            eng.tensor_tensor(part[c][:], prod[c][:], base_t[:, c * C : (c + 1) * C], ALU.add)
+
+        def fin(c):
+            nc.vector.tensor_tensor(res[c][:], part[c][:], page_a[:, c * C : (c + 1) * C], ALU.add)
+            nc.sync.dma_start(out[:, c * C : (c + 1) * C], res[c][:])
+
+        for c in range(3):
+            mul(nc.gpsimd, c)
+            addb(nc.gpsimd, c)
+        mul(nc.vector, 3)
+        fin(0)
+        addb(nc.vector, 3)
+        fin(1)
+        fin(2)
+        fin(3)

@@ -1,6 +1,7 @@
 from contextlib import ExitStack
 
 import concourse.mybir as mybir
+from concourse.masks import make_identity
 
 K, R, T, J, U = 512, 128, 2048, 512, 1024
 FLOPS = 2 * 2 * K * R * J
@@ -28,94 +29,106 @@ def tile_attend_tcgroundgate_kernel(tc, dtab_words, dtab_scales, tab_words, tab_
 
         offs_t = sb.tile([P, J // 16], U16, name="offs_t")
         offs2_t = sb.tile([P, J // 16], U16, name="offs2_t")
-        tw = sb.tile([P, T], U16, name="tw")
-        dw = sb.tile([P, T], U16, name="dw")
+        tw = sb.tile([P, T], U16, name="tw", tag="big_t")
+        dw = sb.tile([P, T], U16, name="dw", tag="big_d")
         ts = sb.tile([P, T], U8, name="ts")
         ds = sb.tile([P, T], U8, name="ds")
         w_raw = sb.tile([P, 4, R], F32, name="w_raw")
         gain_t = sb.tile([P, 1], F32, name="gain_t")
         og_t = sb.tile([P, 1], F32, name="og_t")
-        ground_t = sb.tile([P, U], F32, name="ground_t")
-        base_t = sb.tile([P, U], F32, name="base_t")
         page_a = sb.tile([P, U], F32, name="page_a")
         page_b = sb.tile([P, U], F32, name="page_b")
+        ident = sb.tile([P, P], F32, name="ident")
 
         nc.vector.memset(ts[:].bitcast(I32), 0)
+        nc.vector.memset(page_a[:], 0.0)
         nc.vector.memset(ds[:].bitcast(I32), 0)
         nc.vector.memset(page_b[:], 0.0)
-        nc.vector.memset(page_a[:], 0.0)
 
         nc.sync.dma_start(offs_t[:], offs)
         nc.sync.dma_start(tw[:].bitcast(I32), tab_words[0].bitcast(I32))
         nc.sync.dma_start(w_raw[:], w1.rearrange("(p j) r -> p j r", j=4))
+        nc.sync.dma_start(dw[:].bitcast(I32), dtab_words[0].bitcast(I32))
         for q in range(4):
             nc.scalar.dma_start(ts[32 * q : 32 * q + 4, :].bitcast(I32), tab_scales[0, 4 * q : 4 * q + 4, :].bitcast(I32))
-        nc.sync.dma_start(dw[:].bitcast(I32), dtab_words[0].bitcast(I32))
         nc.gpsimd.dma_start(gain_t[:], gain)
         nc.gpsimd.dma_start(og_t[:], og)
         for q in range(4):
             nc.sync.dma_start(ds[32 * q : 32 * q + 4, :].bitcast(I32), dtab_scales[0, 4 * q : 4 * q + 4, :].bitcast(I32))
         nc.sync.dma_start(offs2_t[:], offs2)
-        nc.sync.dma_start(ground_t[:], ground)
-        nc.sync.dma_start(base_t[:], base)
+        make_identity(nc, ident[:])
 
-        w_bf = sb.tile([P, R, 4], BF16, name="w_bf", align_bytes=64)
+        w_bf = sb.tile([P, R, 4], BF16, name="w_bf", tag="stage", align_bytes=64)
         w_q = sb.tile([P, R], U32, name="w_q", align_bytes=64)
         w_s = sb.tile([P, R], U8, name="w_s", align_bytes=64)
         nc.scalar.copy(w_bf[:], w_raw[:].rearrange("p j r -> p r j"))
-        gg = sb.tile([P, 1], F32, name="gg")
+        gg = sb.tile([P, 1], F32, name="gg", tag="gg")
         nc.gpsimd.tensor_tensor(gg[:], gain_t[:], og_t[:], ALU.mult)
 
         gts = sb.tile([P, J], U8, name="gts", align_bytes=64)
         gtw = sb.tile([P, J], U16, name="gtw", align_bytes=64)
-        nc.vector.tensor_copy(gts[:], ts[:].indirect(offs_t[:]))
         nc.vector.tensor_copy(gtw[:], tw[:].indirect(offs_t[:]))
+        base_t = sb.tile([P, U], F32, name="base_t", tag="big_t")
+        nc.sync.dma_start(base_t[:], base)
+        nc.vector.tensor_copy(gts[:], ts[:].indirect(offs_t[:]))
         nc.vector.quantize_mx(out=w_q[:].bitcast(FP8X4), scales=w_s[:], in_=w_bf[:].rearrange("p r j -> p (r j)"))
         acc_a = ps.tile([P, J], F32, name="acc_a")
         nc.tensor.matmul_mx(out=acc_a[:], lhsT=w_q[:].bitcast(FP8X4), lhsT_scale=w_s[:], rhs=gtw[:].bitcast(FP4X4), rhs_scale=gts[:], start=True, stop=True)
         sig = sb.tile([P, J], F32, name="sig")
-        sq = sb.tile([P, J], F32, name="sq")
         slope = sb.tile([P, J], F32, name="slope")
         nc.scalar.activation(sig[:], acc_a[:], ACT.Sigmoid, scale=gain_t[:])
-        nc.scalar.activation(sq[:], sig[:], ACT.Square, bias=-0.5)
-        nc.scalar.activation(slope[:], sq[:], ACT.Copy, scale=-1.0, bias=0.25)
 
         xa = sb.tile([P, J], F32, name="xa")
         for h in range(2):
             cols = slice(h * H // 16, (h + 1) * H // 16)
             gds = sb.tile([P, H], U8, name="gds%d" % h, align_bytes=64)
-            gdw = sb.tile([P, H], U16, name="gdw%d" % h, align_bytes=64)
-            nc.vector.tensor_copy(gds[:], ds[:].indirect(offs_t[:, cols]))
+            gdw = sb.tile([P, H], U16, name="gdw%d" % h, tag="stage" if h == 0 else "gdw1", align_bytes=64)
             nc.vector.tensor_copy(gdw[:], dw[:].indirect(offs_t[:, cols]))
+            nc.vector.tensor_copy(gds[:], ds[:].indirect(offs_t[:, cols]))
             acc_d = ps.tile([P, H], F32, name="acc_d%d" % h)
             nc.tensor.matmul_mx(out=acc_d[:], lhsT=w_q[:].bitcast(FP8X4), lhsT_scale=w_s[:], rhs=gdw[:].bitcast(FP4X4), rhs_scale=gds[:], start=True, stop=True)
             nc.scalar.activation(xa[:, h * H : (h + 1) * H], acc_d[:], ACT.Copy, scale=gg[:])
+        ground_t = sb.tile([P, U], F32, name="ground_t", tag="big_d")
+        nc.sync.dma_start(ground_t[:], ground)
+
+        sq = sb.tile([P, J], F32, name="sq", tag="gg")
+        nc.scalar.activation(sq[:], sig[:], ACT.Square, bias=-0.5)
+        nc.scalar.activation(slope[:], sq[:], ACT.Copy, scale=-1.0, bias=0.25)
 
         for h in range(2):
             cols = slice(h * H // 16, (h + 1) * H // 16)
-            nc.vector.tensor_tensor(page_b[:].indirect(offs2_t[:, cols]), xa[:, h * H : (h + 1) * H], slope[:, h * H : (h + 1) * H], ALU.mult)
-        nc.vector.tensor_copy(page_a[:].indirect(offs2_t[:]), xa[:])
+            nc.vector.tensor_copy(page_a[:].indirect(offs2_t[:, cols]), xa[:, h * H : (h + 1) * H])
+        nc.vector.tensor_tensor(page_b[:].indirect(offs2_t[:]), xa[:], slope[:], ALU.mult)
+
+        turned = []
+        for h in range(2):
+            bank = ps.tile([P, 4 * P], F32, name="turn%d" % h)
+            for i in range(4):
+                cols = slice((4 * h + i) * P, (4 * h + i + 1) * P)
+                nc.tensor.matmul(bank[:, i * P : (i + 1) * P], base_t[:, cols], ident[:], is_transpose=True, start=True, stop=False)
+                nc.tensor.matmul(bank[:, i * P : (i + 1) * P], page_a[:, cols], ident[:], is_transpose=True, start=False, stop=True)
+            tt = sb.tile([P, 4 * P], F32, name="turned%d" % h)
+            nc.scalar.copy(tt[:], bank[:])
+            turned.append(tt)
+        sums = []
+        for h in range(2):
+            bank = ps.tile([P, 4 * P], F32, name="back%d" % h)
+            for i in range(4):
+                nc.tensor.transpose(bank[:, i * P : (i + 1) * P], turned[h][:, i * P : (i + 1) * P], ident[:])
+            sums.append(bank)
 
         prod = [sb.tile([P, C], F32, name="prod%d" % c) for c in range(4)]
-        part = [sb.tile([P, C], F32, name="part%d" % c) for c in range(4)]
         res = [sb.tile([P, C], F32, name="res%d" % c) for c in range(4)]
 
-        def mul(eng, c):
-            eng.tensor_tensor(prod[c][:], page_b[:, c * C : (c + 1) * C], ground_t[:, c * C : (c + 1) * C], ALU.mult)
-
-        def addb(eng, c):
-            eng.tensor_tensor(part[c][:], prod[c][:], base_t[:, c * C : (c + 1) * C], ALU.add)
+        def mul(c):
+            nc.vector.tensor_tensor(prod[c][:], page_b[:, c * C : (c + 1) * C], ground_t[:, c * C : (c + 1) * C], ALU.mult)
 
         def fin(c):
-            nc.vector.tensor_tensor(res[c][:], part[c][:], page_a[:, c * C : (c + 1) * C], ALU.add)
+            nc.vector.tensor_tensor(res[c][:], prod[c][:], sums[c // 2][:, (c % 2) * C : (c % 2 + 1) * C], ALU.add)
             nc.sync.dma_start(out[:, c * C : (c + 1) * C], res[c][:])
 
-        for c in range(3):
-            mul(nc.gpsimd, c)
-            addb(nc.gpsimd, c)
-        mul(nc.vector, 3)
-        fin(0)
-        addb(nc.vector, 3)
-        fin(1)
-        fin(2)
+        mul(0)
+        for c in range(1, 4):
+            mul(c)
+            fin(c - 1)
         fin(3)

@@ -41,24 +41,24 @@ def tile_attend_tcgroundgate_kernel(tc, dtab_words, dtab_scales, tab_words, tab_
         ident = sb.tile([P, P], F32, name="ident")
 
         nc.vector.memset(ts[:].bitcast(I32), 0)
-        nc.vector.memset(page_a[:], 0.0)
         nc.vector.memset(ds[:].bitcast(I32), 0)
+        nc.vector.memset(page_a[:], 0.0)
         nc.vector.memset(page_b[:], 0.0)
 
         nc.sync.dma_start(offs_t[:], offs)
         nc.sync.dma_start(tw[:].bitcast(I32), tab_words[0].bitcast(I32))
         nc.sync.dma_start(w_raw[:], w1.rearrange("(p j) r -> p j r", j=4))
+        nc.sync.dma_start(offs2_t[:], offs2)
+        for q in range(4):
+            nc.sync.dma_start(ts[32 * q : 32 * q + 4, :].bitcast(I32), tab_scales[0, 4 * q : 4 * q + 4, :].bitcast(I32))
         nc.sync.dma_start(dw[:].bitcast(I32), dtab_words[0].bitcast(I32))
         for q in range(4):
-            nc.scalar.dma_start(ts[32 * q : 32 * q + 4, :].bitcast(I32), tab_scales[0, 4 * q : 4 * q + 4, :].bitcast(I32))
+            nc.sync.dma_start(ds[32 * q : 32 * q + 4, :].bitcast(I32), dtab_scales[0, 4 * q : 4 * q + 4, :].bitcast(I32))
         nc.gpsimd.dma_start(gain_t[:], gain)
         nc.gpsimd.dma_start(og_t[:], og)
-        for q in range(4):
-            nc.sync.dma_start(ds[32 * q : 32 * q + 4, :].bitcast(I32), dtab_scales[0, 4 * q : 4 * q + 4, :].bitcast(I32))
-        nc.sync.dma_start(offs2_t[:], offs2)
         make_identity(nc, ident[:])
 
-        w_bf = sb.tile([P, R, 4], BF16, name="w_bf", tag="stage", align_bytes=64)
+        w_bf = sb.tile([P, R, 4], BF16, name="w_bf", align_bytes=64)
         w_q = sb.tile([P, R], U32, name="w_q", align_bytes=64)
         w_s = sb.tile([P, R], U8, name="w_s", align_bytes=64)
         nc.scalar.copy(w_bf[:], w_raw[:].rearrange("p j r -> p r j"))
@@ -82,7 +82,7 @@ def tile_attend_tcgroundgate_kernel(tc, dtab_words, dtab_scales, tab_words, tab_
         for h in range(2):
             cols = slice(h * H // 16, (h + 1) * H // 16)
             gds = sb.tile([P, H], U8, name="gds%d" % h, align_bytes=64)
-            gdw = sb.tile([P, H], U16, name="gdw%d" % h, tag="stage" if h == 0 else "gdw1", align_bytes=64)
+            gdw = sb.tile([P, H], U16, name="gdw%d" % h, tag="gdw", align_bytes=64)
             nc.vector.tensor_copy(gdw[:], dw[:].indirect(offs_t[:, cols]))
             nc.vector.tensor_copy(gds[:], ds[:].indirect(offs_t[:, cols]))
             acc_d = ps.tile([P, H], F32, name="acc_d%d" % h)
@@ -117,15 +117,18 @@ def tile_attend_tcgroundgate_kernel(tc, dtab_words, dtab_scales, tab_words, tab_
                 nc.tensor.transpose(bank[:, i * P : (i + 1) * P], turned[h][:, i * P : (i + 1) * P], ident[:])
             sums.append(bank)
 
-        prod = [sb.tile([P, C], F32, name="prod%d" % c) for c in range(4)]
-        res = [sb.tile([P, C], F32, name="res%d" % c) for c in range(4)]
+        edges = [0, 512, 768, 896, 1024]
+        prod = [sb.tile([P, edges[c + 1] - edges[c]], F32, name="prod%d" % c) for c in range(4)]
+        res = [sb.tile([P, edges[c + 1] - edges[c]], F32, name="res%d" % c) for c in range(4)]
 
         def mul(c):
-            nc.vector.tensor_tensor(prod[c][:], page_b[:, c * C : (c + 1) * C], ground_t[:, c * C : (c + 1) * C], ALU.mult)
+            cols = slice(edges[c], edges[c + 1])
+            nc.vector.tensor_tensor(prod[c][:], page_b[:, cols], ground_t[:, cols], ALU.mult)
 
         def fin(c):
-            nc.vector.tensor_tensor(res[c][:], prod[c][:], sums[c // 2][:, (c % 2) * C : (c % 2 + 1) * C], ALU.add)
-            nc.sync.dma_start(out[:, c * C : (c + 1) * C], res[c][:])
+            h = edges[c] // 512
+            nc.vector.tensor_tensor(res[c][:], prod[c][:], sums[h][:, edges[c] - 512 * h : edges[c + 1] - 512 * h], ALU.add)
+            nc.sync.dma_start(out[:, edges[c] : edges[c + 1]], res[c][:])
 
         mul(0)
         for c in range(1, 4):

@@ -29,10 +29,10 @@ def tile_attend_tcgroundgate_kernel(tc, dtab_words, dtab_scales, tab_words, tab_
 
         offs_t = sb.tile([P, J // 16], U16, name="offs_t")
         offs2_t = sb.tile([P, J // 16], U16, name="offs2_t")
-        tw = sb.tile([P, T], U16, name="tw", tag="big_t")
         dw = sb.tile([P, T], U16, name="dw", tag="big_d")
-        ts = sb.tile([P, T], U8, name="ts")
+        tw = sb.tile([P, T], U16, name="tw", tag="big_t")
         ds = sb.tile([P, T], U8, name="ds")
+        ts = sb.tile([P, T], U8, name="ts")
         w_raw = sb.tile([P, 4, R], F32, name="w_raw")
         gain_t = sb.tile([P, 1], F32, name="gain_t")
         og_t = sb.tile([P, 1], F32, name="og_t")
@@ -40,20 +40,20 @@ def tile_attend_tcgroundgate_kernel(tc, dtab_words, dtab_scales, tab_words, tab_
         page_b = sb.tile([P, U], F32, name="page_b")
         ident = sb.tile([P, P], F32, name="ident")
 
-        nc.vector.memset(ts[:].bitcast(I32), 0)
         nc.vector.memset(ds[:].bitcast(I32), 0)
+        nc.vector.memset(ts[:].bitcast(I32), 0)
         nc.vector.memset(page_a[:], 0.0)
         nc.vector.memset(page_b[:], 0.0)
 
         nc.sync.dma_start(offs_t[:], offs)
-        nc.sync.dma_start(tw[:].bitcast(I32), tab_words[0].bitcast(I32))
-        nc.sync.dma_start(w_raw[:], w1.rearrange("(p j) r -> p j r", j=4))
-        nc.sync.dma_start(offs2_t[:], offs2)
-        for q in range(4):
-            nc.sync.dma_start(ts[32 * q : 32 * q + 4, :].bitcast(I32), tab_scales[0, 4 * q : 4 * q + 4, :].bitcast(I32))
         nc.sync.dma_start(dw[:].bitcast(I32), dtab_words[0].bitcast(I32))
+        nc.sync.dma_start(w_raw[:], w1.rearrange("(p j) r -> p j r", j=4))
         for q in range(4):
             nc.sync.dma_start(ds[32 * q : 32 * q + 4, :].bitcast(I32), dtab_scales[0, 4 * q : 4 * q + 4, :].bitcast(I32))
+        nc.sync.dma_start(tw[:].bitcast(I32), tab_words[0].bitcast(I32))
+        for q in range(4):
+            nc.sync.dma_start(ts[32 * q : 32 * q + 4, :].bitcast(I32), tab_scales[0, 4 * q : 4 * q + 4, :].bitcast(I32))
+        nc.sync.dma_start(offs2_t[:], offs2)
         nc.gpsimd.dma_start(gain_t[:], gain)
         nc.gpsimd.dma_start(og_t[:], og)
         make_identity(nc, ident[:])
@@ -62,42 +62,37 @@ def tile_attend_tcgroundgate_kernel(tc, dtab_words, dtab_scales, tab_words, tab_
         w_q = sb.tile([P, R], U32, name="w_q", align_bytes=64)
         w_s = sb.tile([P, R], U8, name="w_s", align_bytes=64)
         nc.scalar.copy(w_bf[:], w_raw[:].rearrange("p j r -> p r j"))
-        gg = sb.tile([P, 1], F32, name="gg", tag="gg")
+        gg = sb.tile([P, 1], F32, name="gg")
         nc.gpsimd.tensor_tensor(gg[:], gain_t[:], og_t[:], ALU.mult)
 
-        gts = sb.tile([P, J], U8, name="gts", align_bytes=64)
-        gtw = sb.tile([P, J], U16, name="gtw", align_bytes=64)
-        nc.vector.tensor_copy(gtw[:], tw[:].indirect(offs_t[:]))
-        base_t = sb.tile([P, U], F32, name="base_t", tag="big_t")
-        nc.sync.dma_start(base_t[:], base)
-        nc.vector.tensor_copy(gts[:], ts[:].indirect(offs_t[:]))
+        gdw = sb.tile([P, J], U16, name="gdw", align_bytes=64)
+        gds = sb.tile([P, J], U8, name="gds", align_bytes=64)
+        nc.vector.tensor_copy(gdw[:], dw[:].indirect(offs_t[:]))
+        nc.vector.tensor_copy(gds[:], ds[:].indirect(offs_t[:]))
         nc.vector.quantize_mx(out=w_q[:].bitcast(FP8X4), scales=w_s[:], in_=w_bf[:].rearrange("p r j -> p (r j)"))
+        acc_d = ps.tile([P, J], F32, name="acc_d")
+        nc.tensor.matmul_mx(out=acc_d[:], lhsT=w_q[:].bitcast(FP8X4), lhsT_scale=w_s[:], rhs=gdw[:].bitcast(FP4X4), rhs_scale=gds[:], start=True, stop=True)
+        base_t = sb.tile([P, U], F32, name="base_t", tag="big_d")
+        nc.sync.dma_start(base_t[:], base)
+        xa = sb.tile([P, J], F32, name="xa")
+        nc.scalar.activation(xa[:], acc_d[:], ACT.Copy, scale=gg[:])
+
+        gtw = sb.tile([P, J], U16, name="gtw", align_bytes=64)
+        gts = sb.tile([P, J], U8, name="gts", align_bytes=64)
+        nc.vector.tensor_copy(gtw[:], tw[:].indirect(offs_t[:]))
+        nc.vector.tensor_copy(gts[:], ts[:].indirect(offs_t[:]))
+        ground_t = sb.tile([P, U], F32, name="ground_t", tag="big_t")
+        nc.sync.dma_start(ground_t[:], ground)
         acc_a = ps.tile([P, J], F32, name="acc_a")
         nc.tensor.matmul_mx(out=acc_a[:], lhsT=w_q[:].bitcast(FP8X4), lhsT_scale=w_s[:], rhs=gtw[:].bitcast(FP4X4), rhs_scale=gts[:], start=True, stop=True)
         sig = sb.tile([P, J], F32, name="sig")
+        sq = sb.tile([P, J], F32, name="sq")
         slope = sb.tile([P, J], F32, name="slope")
         nc.scalar.activation(sig[:], acc_a[:], ACT.Sigmoid, scale=gain_t[:])
-
-        xa = sb.tile([P, J], F32, name="xa")
-        for h in range(2):
-            cols = slice(h * H // 16, (h + 1) * H // 16)
-            gds = sb.tile([P, H], U8, name="gds%d" % h, align_bytes=64)
-            gdw = sb.tile([P, H], U16, name="gdw%d" % h, tag="gdw", align_bytes=64)
-            nc.vector.tensor_copy(gdw[:], dw[:].indirect(offs_t[:, cols]))
-            nc.vector.tensor_copy(gds[:], ds[:].indirect(offs_t[:, cols]))
-            acc_d = ps.tile([P, H], F32, name="acc_d%d" % h)
-            nc.tensor.matmul_mx(out=acc_d[:], lhsT=w_q[:].bitcast(FP8X4), lhsT_scale=w_s[:], rhs=gdw[:].bitcast(FP4X4), rhs_scale=gds[:], start=True, stop=True)
-            nc.scalar.activation(xa[:, h * H : (h + 1) * H], acc_d[:], ACT.Copy, scale=gg[:])
-        ground_t = sb.tile([P, U], F32, name="ground_t", tag="big_d")
-        nc.sync.dma_start(ground_t[:], ground)
-
-        sq = sb.tile([P, J], F32, name="sq", tag="gg")
         nc.scalar.activation(sq[:], sig[:], ACT.Square, bias=-0.5)
         nc.scalar.activation(slope[:], sq[:], ACT.Copy, scale=-1.0, bias=0.25)
 
-        for h in range(2):
-            cols = slice(h * H // 16, (h + 1) * H // 16)
-            nc.vector.tensor_copy(page_a[:].indirect(offs2_t[:, cols]), xa[:, h * H : (h + 1) * H])
+        nc.vector.tensor_copy(page_a[:].indirect(offs2_t[:]), xa[:])
         nc.vector.tensor_tensor(page_b[:].indirect(offs2_t[:]), xa[:], slope[:], ALU.mult)
 
         turned = []

@@ -16,9 +16,20 @@ FP8X4 = mybir.dt.float8_e4m3fn_x4
 FP4X4 = mybir.dt.float4_e2m1fn_x4
 ACT = mybir.ActivationFunctionType
 ALU = mybir.AluOpType
+
 P = 128
-H = J // 2
-C = 256
+PACK = 4
+QUADRANT = 32
+SCALE_ROWS = 4
+BANK = 512
+CHUNK = 256
+EDGES = list(range(0, U + 1, CHUNK))
+
+
+def load_scales(nc, scale_tile, scales):
+    for q in range(P // QUADRANT):
+        rows = scales[0, SCALE_ROWS * q : SCALE_ROWS * (q + 1), :]
+        nc.sync.dma_start(scale_tile[QUADRANT * q : QUADRANT * q + SCALE_ROWS, :].bitcast(I32), rows.bitcast(I32))
 
 
 def tile_attend_tcgroundgate_kernel(tc, dtab_words, dtab_scales, tab_words, tab_scales, w1, gain, ground, og, base, offs, offs2, out):
@@ -29,104 +40,114 @@ def tile_attend_tcgroundgate_kernel(tc, dtab_words, dtab_scales, tab_words, tab_
 
         offs_t = sb.tile([P, J // 16], U16, name="offs_t")
         offs2_t = sb.tile([P, J // 16], U16, name="offs2_t")
-        dw = sb.tile([P, T], U16, name="dw", tag="big_d")
-        tw = sb.tile([P, T], U16, name="tw", tag="big_t")
-        ds = sb.tile([P, T], U8, name="ds")
-        ts = sb.tile([P, T], U8, name="ts")
-        w_raw = sb.tile([P, 4, R], F32, name="w_raw")
+        d_words = sb.tile([P, T], U16, name="d_words", tag="big_d")
+        t_words = sb.tile([P, T], U16, name="t_words", tag="big_t")
+        d_scales = sb.tile([P, T], U8, name="d_scales")
+        t_scales = sb.tile([P, T], U8, name="t_scales")
+        w_raw = sb.tile([P, PACK, R], F32, name="w_raw")
         gain_t = sb.tile([P, 1], F32, name="gain_t")
         og_t = sb.tile([P, 1], F32, name="og_t")
-        page_a = sb.tile([P, U], F32, name="page_a")
-        page_b = sb.tile([P, U], F32, name="page_b")
+        page_lin = sb.tile([P, U], F32, name="page_lin")
+        page_gate = sb.tile([P, U], F32, name="page_gate")
         ident = sb.tile([P, P], F32, name="ident")
 
-        nc.vector.memset(ds[:].bitcast(I32), 0)
-        nc.vector.memset(ts[:].bitcast(I32), 0)
-        nc.vector.memset(page_a[:], 0.0)
-        nc.vector.memset(page_b[:], 0.0)
+        nc.vector.memset(d_scales[:].bitcast(I32), 0)
+        nc.vector.memset(t_scales[:].bitcast(I32), 0)
+        nc.vector.memset(page_lin[:], 0.0)
+        nc.vector.memset(page_gate[:], 0.0)
 
         nc.sync.dma_start(offs_t[:], offs)
-        nc.sync.dma_start(dw[:].bitcast(I32), dtab_words[0].bitcast(I32))
-        nc.sync.dma_start(w_raw[:], w1.rearrange("(p j) r -> p j r", j=4))
-        for q in range(4):
-            nc.sync.dma_start(ds[32 * q : 32 * q + 4, :].bitcast(I32), dtab_scales[0, 4 * q : 4 * q + 4, :].bitcast(I32))
-        nc.sync.dma_start(tw[:].bitcast(I32), tab_words[0].bitcast(I32))
-        for q in range(4):
-            nc.sync.dma_start(ts[32 * q : 32 * q + 4, :].bitcast(I32), tab_scales[0, 4 * q : 4 * q + 4, :].bitcast(I32))
+        nc.sync.dma_start(d_words[:].bitcast(I32), dtab_words[0].bitcast(I32))
+        nc.sync.dma_start(w_raw[:], w1.rearrange("(p j) r -> p j r", j=PACK))
+        load_scales(nc, d_scales, dtab_scales)
+        nc.sync.dma_start(t_words[:].bitcast(I32), tab_words[0].bitcast(I32))
+        load_scales(nc, t_scales, tab_scales)
         nc.sync.dma_start(offs2_t[:], offs2)
         nc.gpsimd.dma_start(gain_t[:], gain)
         nc.gpsimd.dma_start(og_t[:], og)
         make_identity(nc, ident[:])
 
-        w_bf = sb.tile([P, R, 4], BF16, name="w_bf", align_bytes=64)
-        w_q = sb.tile([P, R], U32, name="w_q", align_bytes=64)
-        w_s = sb.tile([P, R], U8, name="w_s", align_bytes=64)
+        w_bf = sb.tile([P, R, PACK], BF16, name="w_bf", align_bytes=64)
+        w_codes = sb.tile([P, R], U32, name="w_codes", align_bytes=64)
+        w_scales = sb.tile([P, R], U8, name="w_scales", align_bytes=64)
         nc.scalar.copy(w_bf[:], w_raw[:].rearrange("p j r -> p r j"))
-        gg = sb.tile([P, 1], F32, name="gg")
-        nc.gpsimd.tensor_tensor(gg[:], gain_t[:], og_t[:], ALU.mult)
+        gain_og = sb.tile([P, 1], F32, name="gain_og")
+        nc.gpsimd.tensor_tensor(gain_og[:], gain_t[:], og_t[:], ALU.mult)
 
-        gdw = sb.tile([P, J], U16, name="gdw", align_bytes=64)
-        gds = sb.tile([P, J], U8, name="gds", align_bytes=64)
-        nc.vector.tensor_copy(gdw[:], dw[:].indirect(offs_t[:]))
-        nc.vector.tensor_copy(gds[:], ds[:].indirect(offs_t[:]))
-        nc.vector.quantize_mx(out=w_q[:].bitcast(FP8X4), scales=w_s[:], in_=w_bf[:].rearrange("p r j -> p (r j)"))
+        def product(acc, words, scale_bytes):
+            nc.tensor.matmul_mx(
+                out=acc[:],
+                lhsT=w_codes[:].bitcast(FP8X4),
+                lhsT_scale=w_scales[:],
+                rhs=words[:].bitcast(FP4X4),
+                rhs_scale=scale_bytes[:],
+                start=True,
+                stop=True,
+            )
+
+        d_words_g = sb.tile([P, J], U16, name="d_words_g", align_bytes=64)
+        d_scales_g = sb.tile([P, J], U8, name="d_scales_g", align_bytes=64)
+        nc.vector.tensor_copy(d_words_g[:], d_words[:].indirect(offs_t[:]))
+        nc.vector.tensor_copy(d_scales_g[:], d_scales[:].indirect(offs_t[:]))
+        nc.vector.quantize_mx(out=w_codes[:].bitcast(FP8X4), scales=w_scales[:], in_=w_bf[:].rearrange("p r j -> p (r j)"))
         acc_d = ps.tile([P, J], F32, name="acc_d")
-        nc.tensor.matmul_mx(out=acc_d[:], lhsT=w_q[:].bitcast(FP8X4), lhsT_scale=w_s[:], rhs=gdw[:].bitcast(FP4X4), rhs_scale=gds[:], start=True, stop=True)
+        product(acc_d, d_words_g, d_scales_g)
         base_t = sb.tile([P, U], F32, name="base_t", tag="big_d")
         nc.sync.dma_start(base_t[:], base)
-        xa = sb.tile([P, J], F32, name="xa")
-        nc.scalar.activation(xa[:], acc_d[:], ACT.Copy, scale=gg[:])
+        lin = sb.tile([P, J], F32, name="lin")
+        nc.scalar.activation(lin[:], acc_d[:], ACT.Copy, scale=gain_og[:])
 
-        gtw = sb.tile([P, J], U16, name="gtw", align_bytes=64)
-        gts = sb.tile([P, J], U8, name="gts", align_bytes=64)
-        nc.vector.tensor_copy(gtw[:], tw[:].indirect(offs_t[:]))
-        nc.vector.tensor_copy(gts[:], ts[:].indirect(offs_t[:]))
+        t_words_g = sb.tile([P, J], U16, name="t_words_g", align_bytes=64)
+        t_scales_g = sb.tile([P, J], U8, name="t_scales_g", align_bytes=64)
+        nc.vector.tensor_copy(t_words_g[:], t_words[:].indirect(offs_t[:]))
+        nc.vector.tensor_copy(t_scales_g[:], t_scales[:].indirect(offs_t[:]))
         ground_t = sb.tile([P, U], F32, name="ground_t", tag="big_t")
         nc.sync.dma_start(ground_t[:], ground)
         acc_a = ps.tile([P, J], F32, name="acc_a")
-        nc.tensor.matmul_mx(out=acc_a[:], lhsT=w_q[:].bitcast(FP8X4), lhsT_scale=w_s[:], rhs=gtw[:].bitcast(FP4X4), rhs_scale=gts[:], start=True, stop=True)
+        product(acc_a, t_words_g, t_scales_g)
         sig = sb.tile([P, J], F32, name="sig")
-        sq = sb.tile([P, J], F32, name="sq")
+        centred_sq = sb.tile([P, J], F32, name="centred_sq")
         slope = sb.tile([P, J], F32, name="slope")
         nc.scalar.activation(sig[:], acc_a[:], ACT.Sigmoid, scale=gain_t[:])
-        nc.scalar.activation(sq[:], sig[:], ACT.Square, bias=-0.5)
-        nc.scalar.activation(slope[:], sq[:], ACT.Copy, scale=-1.0, bias=0.25)
+        nc.scalar.activation(centred_sq[:], sig[:], ACT.Square, bias=-0.5)
+        nc.scalar.activation(slope[:], centred_sq[:], ACT.Copy, scale=-1.0, bias=0.25)
 
-        nc.vector.tensor_copy(page_a[:].indirect(offs2_t[:]), xa[:])
-        nc.vector.tensor_tensor(page_b[:].indirect(offs2_t[:]), xa[:], slope[:], ALU.mult)
+        nc.vector.tensor_copy(page_lin[:].indirect(offs2_t[:]), lin[:])
+        nc.vector.tensor_tensor(page_gate[:].indirect(offs2_t[:]), lin[:], slope[:], ALU.mult)
 
         turned = []
-        for h in range(2):
-            bank = ps.tile([P, 4 * P], F32, name="turn%d" % h)
-            for i in range(4):
-                cols = slice((4 * h + i) * P, (4 * h + i + 1) * P)
-                nc.tensor.matmul(bank[:, i * P : (i + 1) * P], base_t[:, cols], ident[:], is_transpose=True, start=True, stop=False)
-                nc.tensor.matmul(bank[:, i * P : (i + 1) * P], page_a[:, cols], ident[:], is_transpose=True, start=False, stop=True)
-            tt = sb.tile([P, 4 * P], F32, name="turned%d" % h)
-            nc.scalar.copy(tt[:], bank[:])
-            turned.append(tt)
+        for h in range(U // BANK):
+            turn_bank = ps.tile([P, BANK], F32, name="turn%d" % h)
+            for i in range(BANK // P):
+                part = turn_bank[:, i * P : (i + 1) * P]
+                cols = slice(h * BANK + i * P, h * BANK + (i + 1) * P)
+                nc.tensor.matmul(part, base_t[:, cols], ident[:], is_transpose=True, start=True, stop=False)
+                nc.tensor.matmul(part, page_lin[:, cols], ident[:], is_transpose=True, start=False, stop=True)
+            turned_h = sb.tile([P, BANK], F32, name="turned%d" % h)
+            nc.scalar.copy(turned_h[:], turn_bank[:])
+            turned.append(turned_h)
         sums = []
-        for h in range(2):
-            bank = ps.tile([P, 4 * P], F32, name="back%d" % h)
-            for i in range(4):
-                nc.tensor.transpose(bank[:, i * P : (i + 1) * P], turned[h][:, i * P : (i + 1) * P], ident[:])
-            sums.append(bank)
+        for h in range(U // BANK):
+            sum_bank = ps.tile([P, BANK], F32, name="back%d" % h)
+            for i in range(BANK // P):
+                nc.tensor.transpose(sum_bank[:, i * P : (i + 1) * P], turned[h][:, i * P : (i + 1) * P], ident[:])
+            sums.append(sum_bank)
 
-        edges = [0, 512, 768, 896, 1024]
-        prod = [sb.tile([P, edges[c + 1] - edges[c]], F32, name="prod%d" % c) for c in range(4)]
-        res = [sb.tile([P, edges[c + 1] - edges[c]], F32, name="res%d" % c) for c in range(4)]
+        chunks = len(EDGES) - 1
+        prod = [sb.tile([P, EDGES[c + 1] - EDGES[c]], F32, name="prod%d" % c) for c in range(chunks)]
+        res = [sb.tile([P, EDGES[c + 1] - EDGES[c]], F32, name="res%d" % c) for c in range(chunks)]
 
-        def mul(c):
-            cols = slice(edges[c], edges[c + 1])
-            nc.vector.tensor_tensor(prod[c][:], page_b[:, cols], ground_t[:, cols], ALU.mult)
+        def multiply(c):
+            cols = slice(EDGES[c], EDGES[c + 1])
+            nc.vector.tensor_tensor(prod[c][:], page_gate[:, cols], ground_t[:, cols], ALU.mult)
 
-        def fin(c):
-            h = edges[c] // 512
-            nc.vector.tensor_tensor(res[c][:], prod[c][:], sums[h][:, edges[c] - 512 * h : edges[c + 1] - 512 * h], ALU.add)
-            nc.sync.dma_start(out[:, edges[c] : edges[c + 1]], res[c][:])
+        def add_and_store(c):
+            h = EDGES[c] // BANK
+            nc.vector.tensor_tensor(res[c][:], prod[c][:], sums[h][:, EDGES[c] - BANK * h : EDGES[c + 1] - BANK * h], ALU.add)
+            nc.sync.dma_start(out[:, EDGES[c] : EDGES[c + 1]], res[c][:])
 
-        mul(0)
-        for c in range(1, 4):
-            mul(c)
-            fin(c - 1)
-        fin(3)
+        multiply(0)
+        for c in range(1, chunks):
+            multiply(c)
+            add_and_store(c - 1)
+        add_and_store(chunks - 1)

from contextlib import ExitStack

import concourse.mybir as mybir
from concourse.masks import make_identity

K, R, T, J, U = 512, 128, 2048, 512, 1024
FLOPS = 2 * 2 * K * R * J

F32 = mybir.dt.float32
BF16 = mybir.dt.bfloat16
I32 = mybir.dt.int32
U32 = mybir.dt.uint32
U16 = mybir.dt.uint16
U8 = mybir.dt.uint8
FP8X4 = mybir.dt.float8_e4m3fn_x4
FP4X4 = mybir.dt.float4_e2m1fn_x4
ACT = mybir.ActivationFunctionType
ALU = mybir.AluOpType

P = 128
PACK = 4
QUADRANT = 32
SCALE_ROWS = 4
BANK = 512
CHUNK = 256
EDGES = list(range(0, U + 1, CHUNK))


def load_scales(nc, scale_tile, scales):
    for q in range(P // QUADRANT):
        rows = scales[0, SCALE_ROWS * q : SCALE_ROWS * (q + 1), :]
        nc.sync.dma_start(scale_tile[QUADRANT * q : QUADRANT * q + SCALE_ROWS, :].bitcast(I32), rows.bitcast(I32))


def tile_attend_tcgroundgate_kernel(tc, dtab_words, dtab_scales, tab_words, tab_scales, w1, gain, ground, og, base, offs, offs2, out):
    nc = tc.nc
    with ExitStack() as ctx:
        sb = ctx.enter_context(tc.tile_pool(name="sb", bufs=1))
        ps = ctx.enter_context(tc.psum_pool(name="ps", bufs=1))

        offs_t = sb.tile([P, J // 16], U16, name="offs_t")
        offs2_t = sb.tile([P, J // 16], U16, name="offs2_t")
        d_words = sb.tile([P, T], U16, name="d_words", tag="big_d")
        t_words = sb.tile([P, T], U16, name="t_words", tag="big_t")
        d_scales = sb.tile([P, T], U8, name="d_scales")
        t_scales = sb.tile([P, T], U8, name="t_scales")
        w_raw = sb.tile([P, PACK, R], F32, name="w_raw")
        gain_t = sb.tile([P, 1], F32, name="gain_t")
        og_t = sb.tile([P, 1], F32, name="og_t")
        page_lin = sb.tile([P, U], F32, name="page_lin")
        page_gate = sb.tile([P, U], F32, name="page_gate")
        ident = sb.tile([P, P], F32, name="ident")

        nc.vector.memset(d_scales[:].bitcast(I32), 0)
        nc.vector.memset(t_scales[:].bitcast(I32), 0)
        nc.vector.memset(page_lin[:], 0.0)
        nc.vector.memset(page_gate[:], 0.0)

        nc.sync.dma_start(offs_t[:], offs)
        nc.sync.dma_start(d_words[:].bitcast(I32), dtab_words[0].bitcast(I32))
        nc.sync.dma_start(w_raw[:], w1.rearrange("(p j) r -> p j r", j=PACK))
        load_scales(nc, d_scales, dtab_scales)
        nc.sync.dma_start(t_words[:].bitcast(I32), tab_words[0].bitcast(I32))
        load_scales(nc, t_scales, tab_scales)
        nc.sync.dma_start(offs2_t[:], offs2)
        nc.gpsimd.dma_start(gain_t[:], gain)
        nc.gpsimd.dma_start(og_t[:], og)
        make_identity(nc, ident[:])

        w_bf = sb.tile([P, R, PACK], BF16, name="w_bf", align_bytes=64)
        w_codes = sb.tile([P, R], U32, name="w_codes", align_bytes=64)
        w_scales = sb.tile([P, R], U8, name="w_scales", align_bytes=64)
        nc.scalar.copy(w_bf[:], w_raw[:].rearrange("p j r -> p r j"))
        gain_og = sb.tile([P, 1], F32, name="gain_og")
        nc.gpsimd.tensor_tensor(gain_og[:], gain_t[:], og_t[:], ALU.mult)

        def product(acc, words, scale_bytes):
            nc.tensor.matmul_mx(
                out=acc[:],
                lhsT=w_codes[:].bitcast(FP8X4),
                lhsT_scale=w_scales[:],
                rhs=words[:].bitcast(FP4X4),
                rhs_scale=scale_bytes[:],
                start=True,
                stop=True,
            )

        d_words_g = sb.tile([P, J], U16, name="d_words_g", align_bytes=64)
        d_scales_g = sb.tile([P, J], U8, name="d_scales_g", align_bytes=64)
        nc.vector.tensor_copy(d_words_g[:], d_words[:].indirect(offs_t[:]))
        nc.vector.tensor_copy(d_scales_g[:], d_scales[:].indirect(offs_t[:]))
        nc.vector.quantize_mx(out=w_codes[:].bitcast(FP8X4), scales=w_scales[:], in_=w_bf[:].rearrange("p r j -> p (r j)"))
        acc_d = ps.tile([P, J], F32, name="acc_d")
        product(acc_d, d_words_g, d_scales_g)
        base_t = sb.tile([P, U], F32, name="base_t", tag="big_d")
        nc.sync.dma_start(base_t[:], base)
        lin = sb.tile([P, J], F32, name="lin")
        nc.scalar.activation(lin[:], acc_d[:], ACT.Copy, scale=gain_og[:])

        t_words_g = sb.tile([P, J], U16, name="t_words_g", align_bytes=64)
        t_scales_g = sb.tile([P, J], U8, name="t_scales_g", align_bytes=64)
        nc.vector.tensor_copy(t_words_g[:], t_words[:].indirect(offs_t[:]))
        nc.vector.tensor_copy(t_scales_g[:], t_scales[:].indirect(offs_t[:]))
        ground_t = sb.tile([P, U], F32, name="ground_t", tag="big_t")
        nc.sync.dma_start(ground_t[:], ground)
        acc_a = ps.tile([P, J], F32, name="acc_a")
        product(acc_a, t_words_g, t_scales_g)
        sig = sb.tile([P, J], F32, name="sig")
        centred_sq = sb.tile([P, J], F32, name="centred_sq")
        slope = sb.tile([P, J], F32, name="slope")
        nc.scalar.activation(sig[:], acc_a[:], ACT.Sigmoid, scale=gain_t[:])
        nc.scalar.activation(centred_sq[:], sig[:], ACT.Square, bias=-0.5)
        nc.scalar.activation(slope[:], centred_sq[:], ACT.Copy, scale=-1.0, bias=0.25)

        nc.vector.tensor_copy(page_lin[:].indirect(offs2_t[:]), lin[:])
        nc.vector.tensor_tensor(page_gate[:].indirect(offs2_t[:]), lin[:], slope[:], ALU.mult)

        turned = []
        for h in range(U // BANK):
            turn_bank = ps.tile([P, BANK], F32, name="turn%d" % h)
            for i in range(BANK // P):
                part = turn_bank[:, i * P : (i + 1) * P]
                cols = slice(h * BANK + i * P, h * BANK + (i + 1) * P)
                nc.tensor.matmul(part, base_t[:, cols], ident[:], is_transpose=True, start=True, stop=False)
                nc.tensor.matmul(part, page_lin[:, cols], ident[:], is_transpose=True, start=False, stop=True)
            turned_h = sb.tile([P, BANK], F32, name="turned%d" % h)
            nc.scalar.copy(turned_h[:], turn_bank[:])
            turned.append(turned_h)
        sums = []
        for h in range(U // BANK):
            sum_bank = ps.tile([P, BANK], F32, name="back%d" % h)
            for i in range(BANK // P):
                nc.tensor.transpose(sum_bank[:, i * P : (i + 1) * P], turned[h][:, i * P : (i + 1) * P], ident[:])
            sums.append(sum_bank)

        chunks = len(EDGES) - 1
        prod = [sb.tile([P, EDGES[c + 1] - EDGES[c]], F32, name="prod%d" % c) for c in range(chunks)]
        res = [sb.tile([P, EDGES[c + 1] - EDGES[c]], F32, name="res%d" % c) for c in range(chunks)]

        def multiply(c):
            cols = slice(EDGES[c], EDGES[c + 1])
            nc.vector.tensor_tensor(prod[c][:], page_gate[:, cols], ground_t[:, cols], ALU.mult)

        def add_and_store(c):
            h = EDGES[c] // BANK
            nc.vector.tensor_tensor(res[c][:], prod[c][:], sums[h][:, EDGES[c] - BANK * h : EDGES[c + 1] - BANK * h], ALU.add)
            nc.sync.dma_start(out[:, EDGES[c] : EDGES[c + 1]], res[c][:])

        multiply(0)
        for c in range(1, chunks):
            multiply(c)
            add_and_store(c - 1)
        add_and_store(chunks - 1)
